import numpy as np
import ml_dtypes


def mxq(x, axis, fmt="e4m3"):
    dtype, down = {"e4m3": (ml_dtypes.float8_e4m3fn, 7), "e5m2": (ml_dtypes.float8_e5m2, 14)}[fmt]
    v = np.moveaxis(np.asarray(x, np.float32).astype(ml_dtypes.bfloat16).astype(np.float64), axis, -1)
    blocks = v.reshape(v.shape[:-1] + (-1, 32))
    amax = np.abs(blocks).max(-1, keepdims=True)
    byte = np.maximum(np.where(amax > 0, np.frexp(amax)[1] - 1 + 127, 0) - down, 1)
    scale = np.exp2(byte - 127.0)
    codes = (blocks / scale).astype(np.float32).astype(dtype).astype(np.float64)
    return np.moveaxis((codes * scale).reshape(v.shape), -1, axis)


WIDE = False


def mx_kscale(k):
    if not WIDE:
        return np.ones(k)
    levels = np.array([30, -30])
    if k % 512:
        return np.exp2(np.random.permutation(np.resize(levels, k // 32))).repeat(32)
    a = np.empty((k // 512, 16))
    for p in range(k // 512):
        a[p, :8] = np.random.permutation(np.resize(levels, 8))
        for g in range(8):
            far = levels[np.abs(levels - a[p, g]) >= 10]
            a[p, g + 8] = far[np.random.randint(len(far))]
    return np.exp2(a.ravel()).repeat(32)


def f64(x):
    return np.asarray(x).astype(np.float64)


def striped(idx):
    return np.tile(np.asarray(idx).reshape(-1, 16).T, (8, 1)).astype(np.uint16)


def unstriped(offs):
    return offs[:16].T.reshape(-1).astype(np.int64)


E2M1 = np.array([0.0, 0.5, 1.0, 1.5, 2.0, 3.0, 4.0, 6.0, -0.0, -0.5, -1.0, -1.5, -2.0, -3.0, -4.0, -6.0])


def pack_weight(w, fmt):
    k, n = w.shape
    w = f64(np.asarray(w, np.float32).astype(ml_dtypes.bfloat16)).reshape(k // 32, 32, n)
    amax = np.abs(w).max(1)
    if fmt in ("e4m3", "e5m2"):
        byte = np.frexp(amax)[1] - 1 + 127 - (7 if fmt == "e4m3" else 14)
    else:
        mant, ex = np.frexp(amax / 6.0)
        byte = np.where(mant > 0.5, ex, ex - 1) + 127
    byte = np.clip(np.where(amax > 0, byte, 1), 1, 254)
    scaled = (w * np.exp2(127.0 - byte)[:, None, :]).reshape(k, n).astype(np.float32)
    by_word = np.ascontiguousarray(scaled.reshape(k // 512, 128, 4, n).transpose(0, 1, 3, 2))
    if fmt in ("e4m3", "e5m2"):
        words = by_word.astype(ml_dtypes.float8_e4m3fn if fmt == "e4m3" else ml_dtypes.float8_e5m2).view(np.uint8)
    else:
        c = by_word.astype(ml_dtypes.float4_e2m1fn).view(np.uint8) & 0xF
        words = (c[..., 0::2] | (c[..., 1::2] << 4)).reshape(k // 512, 128, 2 * n)
    return np.ascontiguousarray(words), np.ascontiguousarray(byte.astype(np.uint8).reshape(k // 512, 16, n))


def unpack_weight(words, scales, fmt):
    g, _, n = scales.shape
    words = np.ascontiguousarray(words).reshape(g, 128, n, -1)
    if fmt in ("e4m3", "e5m2"):
        vals = words.view(ml_dtypes.float8_e4m3fn if fmt == "e4m3" else ml_dtypes.float8_e5m2).astype(np.float64)
    else:
        nib = np.empty((g, 128, n, 4), np.uint8)
        nib[..., 0::2] = words & 0xF
        nib[..., 1::2] = words >> 4
        vals = E2M1[nib]
    vals = vals * np.repeat(np.exp2(scales.astype(np.float64) - 127.0), 8, axis=1)[..., None]
    return vals.transpose(0, 1, 3, 2).reshape(g * 512, n)


K, T, J, I, R, E, V = 512, 512, 256, 256, 512, 32, 512


def setup_inputs():
    n = np.random.standard_normal
    idx = np.random.permutation(T)[:J]
    idx2 = np.random.permutation(T)[:I]
    idx3 = np.random.permutation(V)[:I]
    fk = mx_kscale(K)
    fr = mx_kscale(R)
    xtp = pack_weight(n((K, T)) / fk[:, None], "e2m1")
    wap = pack_weight(n((K, R)) * 0.5 / np.sqrt(K) * fk[:, None] * fr, "e2m1")
    wbp = pack_weight(n((K, R)) * 1 / np.sqrt(K) * fk[:, None] / fr, "e5m2")
    return {
        "xt_words": xtp[0],
        "xt_scales": xtp[1],
        "wa_words": wap[0],
        "wa_scales": wap[1],
        "wb_words": wbp[0],
        "wb_scales": wbp[1],
        "tb": (n((R, V)) * 0.5 / fr[:, None]).astype(np.float32),
        "bi": (np.random.uniform(-15.0, 15.0, (1, I))).astype(np.float32),
        "offs": striped(idx),
        "offs2": striped(idx2),
        "offs3": striped(idx3),
    }


def reference(xt_words, xt_scales, wa_words, wa_scales, wb_words, wb_scales, tb, bi, offs, offs2, offs3):
    idx = unstriped(offs)
    idx2 = unstriped(offs2)
    idx3 = unstriped(offs3)
    xtu = unpack_weight(xt_words, xt_scales, "e2m1")
    wau = unpack_weight(wa_words, wa_scales, "e2m1")
    wbu = unpack_weight(wb_words, wb_scales, "e5m2")
    xtidxg = xtu[:, idx]
    za = wau.T @ xtidxg
    ma1 = za.reshape(R, E, J // E).mean(axis=2)
    ma2 = np.repeat(ma1, J // E, axis=1)
    ha = za - ma2
    xtidx2g = xtu[:, idx2]
    zb = wbu.T @ xtidx2g
    hb = np.maximum(zb - f64(tb)[:, idx3], 0.0)
    haq = mxq(ha, 0, "e5m2")
    hbq = mxq(hb, 0, "e4m3")
    a0 = haq.T @ hbq
    a = a0 + f64(bi)
    mn = np.mean(a, axis=1, keepdims=True)
    d = a - mn
    y = d / (np.mean(np.abs(d), axis=1, keepdims=True) + 4.0)
    return y

@@ -1,0 +1,199 @@
+from contextlib import ExitStack
+
+import concourse.mybir as mybir
+
+F32 = mybir.dt.float32
+BF16 = mybir.dt.bfloat16
+I32 = mybir.dt.int32
+U32 = mybir.dt.uint32
+U16 = mybir.dt.uint16
+U8 = mybir.dt.uint8
+E2M1 = mybir.dt.float4_e2m1fn_x4
+E5M2 = mybir.dt.float8_e5m2_x4
+E4M3 = mybir.dt.float8_e4m3fn_x4
+ALU = mybir.AluOpType
+ACT = mybir.ActivationFunctionType
+AXIS = mybir.AxisListType
+
+P = 128
+T = 512
+V = 512
+R = 512
+J = 256
+I = 256
+SLOTS = 4
+BUNDLE = 8
+HALF = 128
+RUN = 8
+
+FLOPS = 2 * 512 * R * J + 2 * 512 * R * I + 2 * R * J * I
+
+
+def tile_list_meet_levelled_overtable_spread_kernel(
+    tc, xt_words, xt_scales, wa_words, wa_scales, wb_words, wb_scales, tb, bi, offs, offs2, offs3, out
+):
+    nc = tc.nc
+    with ExitStack() as ctx:
+        lists = ctx.enter_context(tc.tile_pool(name="lists", bufs=1))
+        sb = ctx.enter_context(tc.tile_pool(name="sb", bufs=1))
+        ps = ctx.enter_context(tc.psum_pool(name="ps", bufs=1))
+
+        def tile(shape, dtype, name):
+            return sb.tile(shape, dtype, name=name, align_bytes=64)
+
+        def load_scales(queues, plane, scales):
+            rows = scales[0].bitcast(I32)
+            for q in range(4):
+                quad = rows[4 * q : 4 * q + 4, :].unsqueeze(0).broadcast_to([8, 4, T // 4])
+                queues[q % len(queues)].dma_start(plane[32 * q : 32 * q + 32, :].bitcast(I32), quad)
+
+        rows_list = lists.tile([P, J // 16], U16, name="rows_list")
+        cols_list = lists.tile([P, I // 16], U16, name="cols_list")
+        table_list = lists.tile([P, I // 16], U16, name="table_list")
+
+        x_words = tile([P, T], U16, "x_words")
+        x_plane = tile([P, T], U8, "x_plane")
+        wa_raw = tile([P, R // 2], U32, "wa_raw")
+        wa_plane_raw = tile([P, R // 4], U32, "wa_plane_raw")
+        wb_raw = tile([P, R], U32, "wb_raw")
+        wb_plane_raw = tile([P, R // 4], U32, "wb_plane_raw")
+        table = [tile([P, V], F32, "table%d" % t) for t in range(SLOTS)]
+        bias = tile([P, I], F32, "bias")
+
+        table_rows = tb.rearrange("(g t q) v -> t g q v", t=SLOTS, q=RUN)
+        nc.sync.dma_start(rows_list[:], offs)
+        nc.scalar.dma_start(x_words[:].bitcast(I32), xt_words[0].bitcast(I32))
+        load_scales([nc.sync, nc.scalar], x_plane, xt_scales)
+        nc.sync.dma_start(wa_raw[:].bitcast(I32), wa_words[0].bitcast(I32))
+        nc.scalar.dma_start(table[0][:], table_rows[0])
+        load_scales([nc.gpsimd], wb_plane_raw, wb_scales)
+        load_scales([nc.sync], wa_plane_raw, wa_scales)
+        nc.sync.dma_start(cols_list[:], offs2)
+        nc.sync.dma_start(table_list[:], offs3)
+        nc.sync.dma_start(wb_raw[:].bitcast(I32), wb_words[0].rearrange("p n t -> p (n t)").bitcast(I32))
+        for t in range(1, SLOTS):
+            nc.sync.dma_start(table[t][:], table_rows[t])
+        nc.sync.dma_start(bias[:], bi[0].partition_broadcast(P))
+
+        dev = [tile([P, I + 8], F32, "dev%d" % h) for h in range(2)]
+        four = tile([P, 1], F32, "four")
+        nc.vector.memset(four[:], 4.0)
+        for h in range(2):
+            nc.scalar.activation(dev[h][:, I : I + 1], four[:], ACT.Copy, scale=float(I * I))
+
+        def deal(name, raw, words_per_run):
+            dealt = tile([P, raw.shape[1]], U32, name)
+            nc.scalar.copy(
+                dealt[:].rearrange("p (t g w) -> p t g w", t=SLOTS, w=words_per_run),
+                raw[:].rearrange("p (g t w) -> p t g w", t=SLOTS, w=words_per_run),
+            )
+            return dealt
+
+        wa = deal("wa", wa_raw, RUN // 2)
+        wa_plane = deal("wa_plane", wa_plane_raw, RUN // 4)
+        wb = deal("wb", wb_raw, RUN)
+        wb_plane = deal("wb_plane", wb_plane_raw, RUN // 4)
+
+        xa = tile([P, J], U16, "xa")
+        xa_plane = tile([P, J], U8, "xa_plane")
+        xb = tile([P, I], U16, "xb")
+        xb_plane = tile([P, I], U8, "xb_plane")
+        nc.vector.tensor_copy(xa[:], x_words[:].indirect(rows_list[:]))
+        nc.vector.tensor_copy(xa_plane[:], x_plane[:].indirect(rows_list[:]))
+        nc.vector.tensor_copy(xb[:], x_words[:].indirect(cols_list[:]))
+        nc.vector.tensor_copy(xb_plane[:], x_plane[:].indirect(cols_list[:]))
+
+        picked = tile([P, SLOTS, I], F32, "picked")
+        for t in range(SLOTS):
+            nc.scalar.activation(picked[:, t, :], table[t][:].indirect(table_list[:]), ACT.Copy)
+
+        def first_product(name, w_codes, w_plane, x_codes, x_scales):
+            banks = []
+            for h in range(2):
+                bank = ps.tile([P, SLOTS, HALF], F32, name="%s%d" % (name, h))
+                cols = slice(h * HALF, (h + 1) * HALF)
+                for t in range(SLOTS):
+                    nc.tensor.matmul_mx(
+                        out=bank[:, t, :],
+                        lhsT=w_codes(t),
+                        lhsT_scale=w_plane[:].bitcast(U8)[:, t * P : (t + 1) * P],
+                        rhs=x_codes[:, cols].bitcast(E2M1),
+                        rhs_scale=x_scales[:, cols],
+                        start=True,
+                        stop=True,
+                    )
+                banks.append(bank)
+            return banks
+
+        za = first_product("za", lambda t: wa[:, t * P // 2 : (t + 1) * P // 2].bitcast(E2M1), wa_plane, xa, xa_plane)
+        zb = first_product("zb", lambda t: wb[:, t * P : (t + 1) * P].bitcast(E5M2), wb_plane, xb, xb_plane)
+
+        bundles = HALF // BUNDLE
+        sums = [tile([P, bundles, SLOTS], F32, "sums%d" % h) for h in range(2)]
+        means = [tile([P, bundles, SLOTS], F32, "means%d" % h) for h in range(2)]
+        for h in range(2):
+            nc.vector.tensor_reduce(
+                sums[h][:], za[h][:].rearrange("p t (e j) -> p e t j", j=BUNDLE), AXIS.X, ALU.add
+            )
+            nc.gpsimd.tensor_scalar(means[h][:], sums[h][:], 1.0 / BUNDLE, 0.0, ALU.mult, ALU.add)
+
+        hb16 = tile([P, I, SLOTS], BF16, "hb16")
+        for h in range(2):
+            diff = tile([P, SLOTS, HALF], F32, "diff%d" % h)
+            nc.vector.tensor_tensor(diff[:], zb[h][:], picked[:, :, h * HALF : (h + 1) * HALF], ALU.subtract)
+            nc.scalar.activation(
+                hb16[:, h * HALF : (h + 1) * HALF, :].rearrange("p (c i) t -> p c t i", i=4),
+                diff[:].rearrange("p t (c i) -> p c t i", i=4),
+                ACT.Relu,
+            )
+
+        hb_codes = tile([P, I], U32, "hb_codes")
+        hb_plane = tile([P, I], U8, "hb_plane")
+        a0 = []
+        for h in range(2):
+            ha16 = tile([P, bundles, BUNDLE, SLOTS], BF16, "ha16_%d" % h)
+            nc.vector.tensor_tensor(
+                ha16[:],
+                za[h][:].rearrange("p t (e j) -> p e j t", j=BUNDLE),
+                means[h][:].unsqueeze(2).broadcast_to([P, bundles, BUNDLE, SLOTS]),
+                ALU.subtract,
+            )
+            if h == 0:
+                nc.vector.quantize_mx(
+                    out=hb_codes[:].bitcast(E4M3), scales=hb_plane[:], in_=hb16[:].rearrange("p i t -> p (i t)")
+                )
+            ha_codes = tile([P, HALF], U32, "ha_codes%d" % h)
+            ha_plane = tile([P, HALF], U8, "ha_plane%d" % h)
+            nc.vector.quantize_mx(
+                out=ha_codes[:].bitcast(E5M2), scales=ha_plane[:], in_=ha16[:].rearrange("p e j t -> p (e j t)")
+            )
+            bank = ps.tile([P, I], F32, name="a0_%d" % h)
+            nc.tensor.matmul_mx(
+                out=bank[:],
+                lhsT=ha_codes[:].bitcast(E5M2),
+                lhsT_scale=ha_plane[:],
+                rhs=hb_codes[:].bitcast(E4M3),
+                rhs_scale=hb_plane[:],
+                start=True,
+                stop=True,
+            )
+            a0.append(bank)
+
+        a = [tile([P, I], F32, "a%d" % h) for h in range(2)]
+        total = [tile([P, 1], F32, "total%d" % h) for h in range(2)]
+        spread = [tile([P, 1], F32, "spread%d" % h) for h in range(2)]
+        inverse = [tile([P, 1], F32, "inverse%d" % h) for h in range(2)]
+        y = [tile([P, I], F32, "y%d" % h) for h in range(2)]
+        for h in range(2):
+            nc.vector.scalar_tensor_tensor(a[h][:], a0[h][:], 1.0, bias[:], ALU.mult, ALU.add, accum_out=total[h][:])
+        for h in range(2):
+            nc.vector.tensor_scalar(dev[h][:, 0:I], a[h][:], float(I), total[h][:], ALU.mult, ALU.subtract)
+        magnitude = tile([P, I + 1], F32, "magnitude")
+        nc.scalar.activation(magnitude[:], dev[0][:, 0 : I + 1], ACT.Abs, accum_out=spread[0][:])
+        nc.vector.tensor_reduce(spread[1][:], dev[1][:, 0 : I + 1], AXIS.X, ALU.add, apply_absolute_value=True)
+        for h in range(2):
+            nc.vector.reciprocal(inverse[h][:], spread[h][:])
+        for h in range(2):
+            nc.vector.tensor_scalar(y[h][:], dev[h][:, 0:I], inverse[h][:], float(I), ALU.mult, ALU.mult)
+            queue = nc.scalar if h == 0 else nc.sync
+            queue.dma_start(out[h * HALF : (h + 1) * HALF, :], y[h][:])

@@ -16,17 +16,23 @@ ACT = mybir.ActivationFunctionType
 AXIS = mybir.AxisListType
 
 P = 128
+K = 512
 T = 512
 V = 512
 R = 512
 J = 256
 I = 256
+LIST_GROUP = 16
 SLOTS = 4
+RUN = 8
 BUNDLE = 8
 HALF = 128
-RUN = 8
+BUNDLES = HALF // BUNDLE
+QUADRANTS = 4
+SCALE_ROWS = 4
+WEAVE = 4
 
-FLOPS = 2 * 512 * R * J + 2 * 512 * R * I + 2 * R * J * I
+FLOPS = 2 * K * R * J + 2 * K * R * I + 2 * R * J * I
 
 
 def tile_list_meet_levelled_overtable_spread_kernel(
@@ -38,18 +44,23 @@ def tile_list_meet_levelled_overtable_spread_kernel(
         sb = ctx.enter_context(tc.tile_pool(name="sb", bufs=1))
         ps = ctx.enter_context(tc.psum_pool(name="ps", bufs=1))
 
-        def tile(shape, dtype, name):
-            return sb.tile(shape, dtype, name=name, align_bytes=64)
+        def tile(shape, dtype, name, tag=None):
+            return sb.tile(shape, dtype, name=name, tag=tag or name, align_bytes=64)
+
+        def half(h):
+            return slice(h * HALF, (h + 1) * HALF)
 
         def load_scales(queues, plane, scales):
             rows = scales[0].bitcast(I32)
-            for q in range(4):
-                quad = rows[4 * q : 4 * q + 4, :].unsqueeze(0).broadcast_to([8, 4, T // 4])
-                queues[q % len(queues)].dma_start(plane[32 * q : 32 * q + 32, :].bitcast(I32), quad)
+            height = P // QUADRANTS
+            for q in range(QUADRANTS):
+                own = rows[SCALE_ROWS * q : SCALE_ROWS * (q + 1), :]
+                repeated = own.unsqueeze(0).broadcast_to([height // SCALE_ROWS, SCALE_ROWS, rows.shape[1]])
+                queues[q % len(queues)].dma_start(plane[height * q : height * (q + 1), :].bitcast(I32), repeated)
 
-        rows_list = lists.tile([P, J // 16], U16, name="rows_list")
-        cols_list = lists.tile([P, I // 16], U16, name="cols_list")
-        table_list = lists.tile([P, I // 16], U16, name="table_list")
+        rows_list = lists.tile([P, J // LIST_GROUP], U16, name="rows_list")
+        cols_list = lists.tile([P, I // LIST_GROUP], U16, name="cols_list")
+        table_list = lists.tile([P, I // LIST_GROUP], U16, name="table_list")
 
         x_words = tile([P, T], U16, "x_words")
         x_plane = tile([P, T], U8, "x_plane")
@@ -57,22 +68,23 @@ def tile_list_meet_levelled_overtable_spread_kernel(
         wa_plane_raw = tile([P, R // 4], U32, "wa_plane_raw")
         wb_raw = tile([P, R], U32, "wb_raw")
         wb_plane_raw = tile([P, R // 4], U32, "wb_plane_raw")
-        table = [tile([P, V], F32, "table%d" % t) for t in range(SLOTS)]
+        table = [tile([P, V], F32, "table%d" % s) for s in range(SLOTS)]
         bias = tile([P, I], F32, "bias")
 
-        table_rows = tb.rearrange("(g t q) v -> t g q v", t=SLOTS, q=RUN)
+        table_rows = tb.rearrange("(g s q) v -> s g q v", s=SLOTS, q=RUN)
+        for s in range(2):
+            nc.gpsimd.dma_start(table[s][:], table_rows[s])
         nc.sync.dma_start(rows_list[:], offs)
+        load_scales([nc.scalar, nc.sync], x_plane, xt_scales)
         nc.scalar.dma_start(x_words[:].bitcast(I32), xt_words[0].bitcast(I32))
-        load_scales([nc.sync, nc.scalar], x_plane, xt_scales)
         nc.sync.dma_start(wa_raw[:].bitcast(I32), wa_words[0].bitcast(I32))
-        nc.scalar.dma_start(table[0][:], table_rows[0])
-        load_scales([nc.gpsimd], wb_plane_raw, wb_scales)
+        nc.scalar.dma_start(wb_raw[:].bitcast(I32), wb_words[0].rearrange("p n t -> p (n t)").bitcast(I32))
         load_scales([nc.sync], wa_plane_raw, wa_scales)
         nc.sync.dma_start(cols_list[:], offs2)
         nc.sync.dma_start(table_list[:], offs3)
-        nc.sync.dma_start(wb_raw[:].bitcast(I32), wb_words[0].rearrange("p n t -> p (n t)").bitcast(I32))
-        for t in range(1, SLOTS):
-            nc.sync.dma_start(table[t][:], table_rows[t])
+        nc.sync.dma_start(table[2][:], table_rows[2])
+        load_scales([nc.sync], wb_plane_raw, wb_scales)
+        nc.sync.dma_start(table[3][:], table_rows[3])
         nc.sync.dma_start(bias[:], bi[0].partition_broadcast(P))
 
         dev = [tile([P, I + 8], F32, "dev%d" % h) for h in range(2)]
@@ -81,18 +93,17 @@ def tile_list_meet_levelled_overtable_spread_kernel(
         for h in range(2):
             nc.scalar.activation(dev[h][:, I : I + 1], four[:], ACT.Copy, scale=float(I * I))
 
-        def deal(name, raw, words_per_run):
+        def deal(name, raw, run_elements):
             dealt = tile([P, raw.shape[1]], U32, name)
             nc.scalar.copy(
-                dealt[:].rearrange("p (t g w) -> p t g w", t=SLOTS, w=words_per_run),
-                raw[:].rearrange("p (g t w) -> p t g w", t=SLOTS, w=words_per_run),
+                dealt[:].rearrange("p (s g w) -> p s g w", s=SLOTS, w=run_elements),
+                raw[:].rearrange("p (g s w) -> p s g w", s=SLOTS, w=run_elements),
             )
             return dealt
 
         wa = deal("wa", wa_raw, RUN // 2)
-        wa_plane = deal("wa_plane", wa_plane_raw, RUN // 4)
         wb = deal("wb", wb_raw, RUN)
-        wb_plane = deal("wb_plane", wb_plane_raw, RUN // 4)
+        wa_plane = deal("wa_plane", wa_plane_raw, RUN // 4)
 
         xa = tile([P, J], U16, "xa")
         xa_plane = tile([P, J], U8, "xa_plane")
@@ -104,96 +115,112 @@ def tile_list_meet_levelled_overtable_spread_kernel(
         nc.vector.tensor_copy(xb_plane[:], x_plane[:].indirect(cols_list[:]))
 
         picked = tile([P, SLOTS, I], F32, "picked")
-        for t in range(SLOTS):
-            nc.scalar.activation(picked[:, t, :], table[t][:].indirect(table_list[:]), ACT.Copy)
 
-        def first_product(name, w_codes, w_plane, x_codes, x_scales):
+        def pick(s):
+            nc.scalar.activation(picked[:, s, :], table[s][:].indirect(table_list[:]), ACT.Copy)
+
+        for s in range(SLOTS - 1):
+            pick(s)
+        wb_plane = deal("wb_plane", wb_plane_raw, RUN // 4)
+        pick(SLOTS - 1)
+
+        def first_product(name, w_words, w_format, w_plane, x_codes, x_scales):
+            width = w_words.shape[1] // SLOTS
             banks = []
             for h in range(2):
                 bank = ps.tile([P, SLOTS, HALF], F32, name="%s%d" % (name, h))
-                cols = slice(h * HALF, (h + 1) * HALF)
-                for t in range(SLOTS):
+                for s in range(SLOTS):
                     nc.tensor.matmul_mx(
-                        out=bank[:, t, :],
-                        lhsT=w_codes(t),
-                        lhsT_scale=w_plane[:].bitcast(U8)[:, t * P : (t + 1) * P],
-                        rhs=x_codes[:, cols].bitcast(E2M1),
-                        rhs_scale=x_scales[:, cols],
+                        out=bank[:, s, :],
+                        lhsT=w_words[:, s * width : (s + 1) * width].bitcast(w_format),
+                        lhsT_scale=w_plane[:].bitcast(U8)[:, s * P : (s + 1) * P],
+                        rhs=x_codes[:, half(h)].bitcast(E2M1),
+                        rhs_scale=x_scales[:, half(h)],
                         start=True,
                         stop=True,
                     )
                 banks.append(bank)
             return banks
 
-        za = first_product("za", lambda t: wa[:, t * P // 2 : (t + 1) * P // 2].bitcast(E2M1), wa_plane, xa, xa_plane)
-        zb = first_product("zb", lambda t: wb[:, t * P : (t + 1) * P].bitcast(E5M2), wb_plane, xb, xb_plane)
+        za = first_product("za", wa, E2M1, wa_plane, xa, xa_plane)
+        zb = first_product("zb", wb, E5M2, wb_plane, xb, xb_plane)
 
-        bundles = HALF // BUNDLE
-        sums = [tile([P, bundles, SLOTS], F32, "sums%d" % h) for h in range(2)]
-        means = [tile([P, bundles, SLOTS], F32, "means%d" % h) for h in range(2)]
+        sums = [tile([P, BUNDLES, SLOTS], F32, "sums%d" % h) for h in range(2)]
+        means = [tile([P, BUNDLES, SLOTS], F32, "means%d" % h) for h in range(2)]
         for h in range(2):
-            nc.vector.tensor_reduce(
-                sums[h][:], za[h][:].rearrange("p t (e j) -> p e t j", j=BUNDLE), AXIS.X, ALU.add
-            )
+            nc.vector.tensor_reduce(sums[h][:], za[h][:].rearrange("p s (e j) -> p e s j", j=BUNDLE), AXIS.X, ALU.add)
             nc.gpsimd.tensor_scalar(means[h][:], sums[h][:], 1.0 / BUNDLE, 0.0, ALU.mult, ALU.add)
 
-        hb16 = tile([P, I, SLOTS], BF16, "hb16")
-        for h in range(2):
-            diff = tile([P, SLOTS, HALF], F32, "diff%d" % h)
-            nc.vector.tensor_tensor(diff[:], zb[h][:], picked[:, :, h * HALF : (h + 1) * HALF], ALU.subtract)
-            nc.scalar.activation(
-                hb16[:, h * HALF : (h + 1) * HALF, :].rearrange("p (c i) t -> p c t i", i=4),
-                diff[:].rearrange("p t (c i) -> p c t i", i=4),
-                ACT.Relu,
-            )
+        ha_plane = [tile([P, HALF], U8, "ha_plane%d" % h) for h in range(2)]
+        hb_codes = [tile([P, HALF], U32, "hb_codes%d" % h) for h in range(2)]
+        hb_plane = [tile([P, HALF], U8, "hb_plane%d" % h) for h in range(2)]
+        ha16 = [tile([P, BUNDLES, BUNDLE, SLOTS], BF16, "ha16_%d" % h) for h in range(2)]
+        hb16 = [tile([P, HALF, SLOTS], BF16, "hb16_%d" % h) for h in range(2)]
 
-        hb_codes = tile([P, I], U32, "hb_codes")
-        hb_plane = tile([P, I], U8, "hb_plane")
-        a0 = []
-        for h in range(2):
-            ha16 = tile([P, bundles, BUNDLE, SLOTS], BF16, "ha16_%d" % h)
+        def level_rows(h):
             nc.vector.tensor_tensor(
-                ha16[:],
-                za[h][:].rearrange("p t (e j) -> p e j t", j=BUNDLE),
-                means[h][:].unsqueeze(2).broadcast_to([P, bundles, BUNDLE, SLOTS]),
+                ha16[h][:],
+                za[h][:].rearrange("p s (e j) -> p e j s", j=BUNDLE),
+                means[h][:].unsqueeze(2).broadcast_to([P, BUNDLES, BUNDLE, SLOTS]),
                 ALU.subtract,
             )
-            if h == 0:
-                nc.vector.quantize_mx(
-                    out=hb_codes[:].bitcast(E4M3), scales=hb_plane[:], in_=hb16[:].rearrange("p i t -> p (i t)")
-                )
-            ha_codes = tile([P, HALF], U32, "ha_codes%d" % h)
-            ha_plane = tile([P, HALF], U8, "ha_plane%d" % h)
-            nc.vector.quantize_mx(
-                out=ha_codes[:].bitcast(E5M2), scales=ha_plane[:], in_=ha16[:].rearrange("p e j t -> p (e j t)")
-            )
-            bank = ps.tile([P, I], F32, name="a0_%d" % h)
-            nc.tensor.matmul_mx(
-                out=bank[:],
-                lhsT=ha_codes[:].bitcast(E5M2),
-                lhsT_scale=ha_plane[:],
-                rhs=hb_codes[:].bitcast(E4M3),
-                rhs_scale=hb_plane[:],
-                start=True,
-                stop=True,
-            )
-            a0.append(bank)
 
-        a = [tile([P, I], F32, "a%d" % h) for h in range(2)]
-        total = [tile([P, 1], F32, "total%d" % h) for h in range(2)]
+        def quantise_rows(h, tag=None):
+            codes = tile([P, HALF], U32, "ha_codes%d" % h, tag)
+            nc.vector.quantize_mx(
+                out=codes[:].bitcast(E5M2), scales=ha_plane[h][:], in_=ha16[h][:].rearrange("p e j s -> p (e j s)")
+            )
+            return codes
+
+        def over_table(h):
+            diff = tile([P, SLOTS, HALF], F32, "diff%d" % h)
+            nc.vector.tensor_tensor(diff[:], zb[h][:], picked[:, :, half(h)], ALU.subtract)
+            woven = hb16[h][:].rearrange("p (c i) s -> p c s i", i=WEAVE)
+            return woven, diff[:].rearrange("p s (c i) -> p c s i", i=WEAVE)
+
+        level_rows(0)
+        ha_codes = [quantise_rows(0)]
+        level_rows(1)
+        woven, planar = over_table(0)
+        nc.scalar.activation(woven, planar, ACT.Relu)
+        woven, planar = over_table(1)
+        ha_codes.append(quantise_rows(1, "picked"))
+        nc.vector.tensor_scalar(woven, planar, 0.0, None, ALU.max)
+        for g in range(2):
+            nc.vector.quantize_mx(
+                out=hb_codes[g][:].bitcast(E4M3), scales=hb_plane[g][:], in_=hb16[g][:].rearrange("p i s -> p (i s)")
+            )
+
+        a0 = [ps.tile([P, I], F32, name="a0_%d" % h) for h in range(2)]
+        for g in range(2):
+            for h in range(2):
+                nc.tensor.matmul_mx(
+                    out=a0[h][:, half(g)],
+                    lhsT=ha_codes[h][:].bitcast(E5M2),
+                    lhsT_scale=ha_plane[h][:],
+                    rhs=hb_codes[g][:].bitcast(E4M3),
+                    rhs_scale=hb_plane[g][:],
+                    start=True,
+                    stop=True,
+                )
+
+        minus_a = [tile([P, I], F32, "minus_a%d" % h) for h in range(2)]
+        minus_total = [tile([P, 1], F32, "minus_total%d" % h) for h in range(2)]
         spread = [tile([P, 1], F32, "spread%d" % h) for h in range(2)]
         inverse = [tile([P, 1], F32, "inverse%d" % h) for h in range(2)]
         y = [tile([P, I], F32, "y%d" % h) for h in range(2)]
         for h in range(2):
-            nc.vector.scalar_tensor_tensor(a[h][:], a0[h][:], 1.0, bias[:], ALU.mult, ALU.add, accum_out=total[h][:])
-        for h in range(2):
-            nc.vector.tensor_scalar(dev[h][:, 0:I], a[h][:], float(I), total[h][:], ALU.mult, ALU.subtract)
+            nc.vector.scalar_tensor_tensor(
+                minus_a[h][:], a0[h][:], -1.0, bias[:], ALU.mult, ALU.subtract, accum_out=minus_total[h][:]
+            )
         magnitude = tile([P, I + 1], F32, "magnitude")
-        nc.scalar.activation(magnitude[:], dev[0][:, 0 : I + 1], ACT.Abs, accum_out=spread[0][:])
+        nc.scalar.activation(dev[0][:, 0:I], minus_a[0][:], ACT.Identity, bias=minus_total[0][:], scale=-float(I))
+        nc.scalar.activation(magnitude[:], dev[0][:, 0 : I + 1], ACT.Abs, scale=1.0 / I, accum_out=spread[0][:])
+        nc.vector.tensor_scalar(dev[1][:, 0:I], minus_a[1][:], -float(I), minus_total[1][:], ALU.mult, ALU.add)
         nc.vector.tensor_reduce(spread[1][:], dev[1][:, 0 : I + 1], AXIS.X, ALU.add, apply_absolute_value=True)
         for h in range(2):
             nc.vector.reciprocal(inverse[h][:], spread[h][:])
-        for h in range(2):
-            nc.vector.tensor_scalar(y[h][:], dev[h][:, 0:I], inverse[h][:], float(I), ALU.mult, ALU.mult)
-            queue = nc.scalar if h == 0 else nc.sync
-            queue.dma_start(out[h * HALF : (h + 1) * HALF, :], y[h][:])
+        nc.scalar.activation(y[0][:], dev[0][:, 0:I], ACT.Copy, scale=inverse[0][:])
+        nc.scalar.dma_start(out[half(0), :], y[0][:])
+        nc.vector.tensor_scalar(y[1][:], dev[1][:, 0:I], inverse[1][:], float(I), ALU.mult, ALU.mult)
+        nc.sync.dma_start(out[half(1), :], y[1][:])

from contextlib import ExitStack

import concourse.mybir as mybir

F32 = mybir.dt.float32
BF16 = mybir.dt.bfloat16
I32 = mybir.dt.int32
U32 = mybir.dt.uint32
U16 = mybir.dt.uint16
U8 = mybir.dt.uint8
E2M1 = mybir.dt.float4_e2m1fn_x4
E5M2 = mybir.dt.float8_e5m2_x4
E4M3 = mybir.dt.float8_e4m3fn_x4
ALU = mybir.AluOpType
ACT = mybir.ActivationFunctionType
AXIS = mybir.AxisListType

P = 128
K = 512
T = 512
V = 512
R = 512
J = 256
I = 256
LIST_GROUP = 16
SLOTS = 4
RUN = 8
BUNDLE = 8
HALF = 128
BUNDLES = HALF // BUNDLE
QUADRANTS = 4
SCALE_ROWS = 4
WEAVE = 4

FLOPS = 2 * K * R * J + 2 * K * R * I + 2 * R * J * I


def tile_list_meet_levelled_overtable_spread_kernel(
    tc, xt_words, xt_scales, wa_words, wa_scales, wb_words, wb_scales, tb, bi, offs, offs2, offs3, out
):
    nc = tc.nc
    with ExitStack() as ctx:
        lists = ctx.enter_context(tc.tile_pool(name="lists", bufs=1))
        sb = ctx.enter_context(tc.tile_pool(name="sb", bufs=1))
        ps = ctx.enter_context(tc.psum_pool(name="ps", bufs=1))

        def tile(shape, dtype, name, tag=None):
            return sb.tile(shape, dtype, name=name, tag=tag or name, align_bytes=64)

        def half(h):
            return slice(h * HALF, (h + 1) * HALF)

        def load_scales(queues, plane, scales):
            rows = scales[0].bitcast(I32)
            height = P // QUADRANTS
            for q in range(QUADRANTS):
                own = rows[SCALE_ROWS * q : SCALE_ROWS * (q + 1), :]
                repeated = own.unsqueeze(0).broadcast_to([height // SCALE_ROWS, SCALE_ROWS, rows.shape[1]])
                queues[q % len(queues)].dma_start(plane[height * q : height * (q + 1), :].bitcast(I32), repeated)

        rows_list = lists.tile([P, J // LIST_GROUP], U16, name="rows_list")
        cols_list = lists.tile([P, I // LIST_GROUP], U16, name="cols_list")
        table_list = lists.tile([P, I // LIST_GROUP], U16, name="table_list")

        x_words = tile([P, T], U16, "x_words")
        x_plane = tile([P, T], U8, "x_plane")
        wa_raw = tile([P, R // 2], U32, "wa_raw")
        wa_plane_raw = tile([P, R // 4], U32, "wa_plane_raw")
        wb_raw = tile([P, R], U32, "wb_raw")
        wb_plane_raw = tile([P, R // 4], U32, "wb_plane_raw")
        table = [tile([P, V], F32, "table%d" % s) for s in range(SLOTS)]
        bias = tile([P, I], F32, "bias")

        table_rows = tb.rearrange("(g s q) v -> s g q v", s=SLOTS, q=RUN)
        for s in range(2):
            nc.gpsimd.dma_start(table[s][:], table_rows[s])
        nc.sync.dma_start(rows_list[:], offs)
        load_scales([nc.scalar, nc.sync], x_plane, xt_scales)
        nc.scalar.dma_start(x_words[:].bitcast(I32), xt_words[0].bitcast(I32))
        nc.sync.dma_start(wa_raw[:].bitcast(I32), wa_words[0].bitcast(I32))
        nc.scalar.dma_start(wb_raw[:].bitcast(I32), wb_words[0].rearrange("p n t -> p (n t)").bitcast(I32))
        load_scales([nc.sync], wa_plane_raw, wa_scales)
        nc.sync.dma_start(cols_list[:], offs2)
        nc.sync.dma_start(table_list[:], offs3)
        nc.sync.dma_start(table[2][:], table_rows[2])
        load_scales([nc.sync], wb_plane_raw, wb_scales)
        nc.sync.dma_start(table[3][:], table_rows[3])
        nc.sync.dma_start(bias[:], bi[0].partition_broadcast(P))

        dev = [tile([P, I + 8], F32, "dev%d" % h) for h in range(2)]
        four = tile([P, 1], F32, "four")
        nc.vector.memset(four[:], 4.0)
        for h in range(2):
            nc.scalar.activation(dev[h][:, I : I + 1], four[:], ACT.Copy, scale=float(I * I))

        def deal(name, raw, run_elements):
            dealt = tile([P, raw.shape[1]], U32, name)
            nc.scalar.copy(
                dealt[:].rearrange("p (s g w) -> p s g w", s=SLOTS, w=run_elements),
                raw[:].rearrange("p (g s w) -> p s g w", s=SLOTS, w=run_elements),
            )
            return dealt

        wa = deal("wa", wa_raw, RUN // 2)
        wb = deal("wb", wb_raw, RUN)
        wa_plane = deal("wa_plane", wa_plane_raw, RUN // 4)

        xa = tile([P, J], U16, "xa")
        xa_plane = tile([P, J], U8, "xa_plane")
        xb = tile([P, I], U16, "xb")
        xb_plane = tile([P, I], U8, "xb_plane")
        nc.vector.tensor_copy(xa[:], x_words[:].indirect(rows_list[:]))
        nc.vector.tensor_copy(xa_plane[:], x_plane[:].indirect(rows_list[:]))
        nc.vector.tensor_copy(xb[:], x_words[:].indirect(cols_list[:]))
        nc.vector.tensor_copy(xb_plane[:], x_plane[:].indirect(cols_list[:]))

        picked = tile([P, SLOTS, I], F32, "picked")

        def pick(s):
            nc.scalar.activation(picked[:, s, :], table[s][:].indirect(table_list[:]), ACT.Copy)

        for s in range(SLOTS - 1):
            pick(s)
        wb_plane = deal("wb_plane", wb_plane_raw, RUN // 4)
        pick(SLOTS - 1)

        def first_product(name, w_words, w_format, w_plane, x_codes, x_scales):
            width = w_words.shape[1] // SLOTS
            banks = []
            for h in range(2):
                bank = ps.tile([P, SLOTS, HALF], F32, name="%s%d" % (name, h))
                for s in range(SLOTS):
                    nc.tensor.matmul_mx(
                        out=bank[:, s, :],
                        lhsT=w_words[:, s * width : (s + 1) * width].bitcast(w_format),
                        lhsT_scale=w_plane[:].bitcast(U8)[:, s * P : (s + 1) * P],
                        rhs=x_codes[:, half(h)].bitcast(E2M1),
                        rhs_scale=x_scales[:, half(h)],
                        start=True,
                        stop=True,
                    )
                banks.append(bank)
            return banks

        za = first_product("za", wa, E2M1, wa_plane, xa, xa_plane)
        zb = first_product("zb", wb, E5M2, wb_plane, xb, xb_plane)

        sums = [tile([P, BUNDLES, SLOTS], F32, "sums%d" % h) for h in range(2)]
        means = [tile([P, BUNDLES, SLOTS], F32, "means%d" % h) for h in range(2)]
        for h in range(2):
            nc.vector.tensor_reduce(sums[h][:], za[h][:].rearrange("p s (e j) -> p e s j", j=BUNDLE), AXIS.X, ALU.add)
            nc.gpsimd.tensor_scalar(means[h][:], sums[h][:], 1.0 / BUNDLE, 0.0, ALU.mult, ALU.add)

        ha_plane = [tile([P, HALF], U8, "ha_plane%d" % h) for h in range(2)]
        hb_codes = [tile([P, HALF], U32, "hb_codes%d" % h) for h in range(2)]
        hb_plane = [tile([P, HALF], U8, "hb_plane%d" % h) for h in range(2)]
        ha16 = [tile([P, BUNDLES, BUNDLE, SLOTS], BF16, "ha16_%d" % h) for h in range(2)]
        hb16 = [tile([P, HALF, SLOTS], BF16, "hb16_%d" % h) for h in range(2)]

        def level_rows(h):
            nc.vector.tensor_tensor(
                ha16[h][:],
                za[h][:].rearrange("p s (e j) -> p e j s", j=BUNDLE),
                means[h][:].unsqueeze(2).broadcast_to([P, BUNDLES, BUNDLE, SLOTS]),
                ALU.subtract,
            )

        def quantise_rows(h, tag=None):
            codes = tile([P, HALF], U32, "ha_codes%d" % h, tag)
            nc.vector.quantize_mx(
                out=codes[:].bitcast(E5M2), scales=ha_plane[h][:], in_=ha16[h][:].rearrange("p e j s -> p (e j s)")
            )
            return codes

        def over_table(h):
            diff = tile([P, SLOTS, HALF], F32, "diff%d" % h)
            nc.vector.tensor_tensor(diff[:], zb[h][:], picked[:, :, half(h)], ALU.subtract)
            woven = hb16[h][:].rearrange("p (c i) s -> p c s i", i=WEAVE)
            return woven, diff[:].rearrange("p s (c i) -> p c s i", i=WEAVE)

        level_rows(0)
        ha_codes = [quantise_rows(0)]
        level_rows(1)
        woven, planar = over_table(0)
        nc.scalar.activation(woven, planar, ACT.Relu)
        woven, planar = over_table(1)
        ha_codes.append(quantise_rows(1, "picked"))
        nc.vector.tensor_scalar(woven, planar, 0.0, None, ALU.max)
        for g in range(2):
            nc.vector.quantize_mx(
                out=hb_codes[g][:].bitcast(E4M3), scales=hb_plane[g][:], in_=hb16[g][:].rearrange("p i s -> p (i s)")
            )

        a0 = [ps.tile([P, I], F32, name="a0_%d" % h) for h in range(2)]
        for g in range(2):
            for h in range(2):
                nc.tensor.matmul_mx(
                    out=a0[h][:, half(g)],
                    lhsT=ha_codes[h][:].bitcast(E5M2),
                    lhsT_scale=ha_plane[h][:],
                    rhs=hb_codes[g][:].bitcast(E4M3),
                    rhs_scale=hb_plane[g][:],
                    start=True,
                    stop=True,
                )

        minus_a = [tile([P, I], F32, "minus_a%d" % h) for h in range(2)]
        minus_total = [tile([P, 1], F32, "minus_total%d" % h) for h in range(2)]
        spread = [tile([P, 1], F32, "spread%d" % h) for h in range(2)]
        inverse = [tile([P, 1], F32, "inverse%d" % h) for h in range(2)]
        y = [tile([P, I], F32, "y%d" % h) for h in range(2)]
        for h in range(2):
            nc.vector.scalar_tensor_tensor(
                minus_a[h][:], a0[h][:], -1.0, bias[:], ALU.mult, ALU.subtract, accum_out=minus_total[h][:]
            )
        magnitude = tile([P, I + 1], F32, "magnitude")
        nc.scalar.activation(dev[0][:, 0:I], minus_a[0][:], ACT.Identity, bias=minus_total[0][:], scale=-float(I))
        nc.scalar.activation(magnitude[:], dev[0][:, 0 : I + 1], ACT.Abs, scale=1.0 / I, accum_out=spread[0][:])
        nc.vector.tensor_scalar(dev[1][:, 0:I], minus_a[1][:], -float(I), minus_total[1][:], ALU.mult, ALU.add)
        nc.vector.tensor_reduce(spread[1][:], dev[1][:, 0 : I + 1], AXIS.X, ALU.add, apply_absolute_value=True)
        for h in range(2):
            nc.vector.reciprocal(inverse[h][:], spread[h][:])
        nc.scalar.activation(y[0][:], dev[0][:, 0:I], ACT.Copy, scale=inverse[0][:])
        nc.scalar.dma_start(out[half(0), :], y[0][:])
        nc.vector.tensor_scalar(y[1][:], dev[1][:, 0:I], inverse[1][:], float(I), ALU.mult, ALU.mult)
        nc.sync.dma_start(out[half(1), :], y[1][:])
